import numpy as np
import ml_dtypes


def mxq(x, axis, fmt="e4m3"):
    dtype, down = {"e4m3": (ml_dtypes.float8_e4m3fn, 7), "e5m2": (ml_dtypes.float8_e5m2, 14)}[fmt]
    v = np.moveaxis(np.asarray(x, np.float32).astype(ml_dtypes.bfloat16).astype(np.float64), axis, -1)
    blocks = v.reshape(v.shape[:-1] + (-1, 32))
    amax = np.abs(blocks).max(-1, keepdims=True)
    byte = np.maximum(np.where(amax > 0, np.frexp(amax)[1] - 1 + 127, 0) - down, 1)
    scale = np.exp2(byte - 127.0)
    codes = (blocks / scale).astype(np.float32).astype(dtype).astype(np.float64)
    return np.moveaxis((codes * scale).reshape(v.shape), -1, axis)


WIDE = False


def mx_kscale(k):
    if not WIDE:
        return np.ones(k)
    levels = np.array([30, -30])
    if k % 512:
        return np.exp2(np.random.permutation(np.resize(levels, k // 32))).repeat(32)
    a = np.empty((k // 512, 16))
    for p in range(k // 512):
        a[p, :8] = np.random.permutation(np.resize(levels, 8))
        for g in range(8):
            far = levels[np.abs(levels - a[p, g]) >= 10]
            a[p, g + 8] = far[np.random.randint(len(far))]
    return np.exp2(a.ravel()).repeat(32)


def f64(x):
    return np.asarray(x).astype(np.float64)


def striped(idx):
    return np.tile(np.asarray(idx).reshape(-1, 16).T, (8, 1)).astype(np.uint16)


def unstriped(offs):
    return offs[:16].T.reshape(-1).astype(np.int64)


E2M1 = np.array([0.0, 0.5, 1.0, 1.5, 2.0, 3.0, 4.0, 6.0, -0.0, -0.5, -1.0, -1.5, -2.0, -3.0, -4.0, -6.0])


def pack_weight(w, fmt):
    k, n = w.shape
    w = f64(np.asarray(w, np.float32).astype(ml_dtypes.bfloat16)).reshape(k // 32, 32, n)
    amax = np.abs(w).max(1)
    if fmt == "e4m3":
        byte = np.frexp(amax)[1] - 1 + 127 - 7
    else:
        mant, ex = np.frexp(amax / 6.0)
        byte = np.where(mant > 0.5, ex, ex - 1) + 127
    byte = np.clip(np.where(amax > 0, byte, 1), 1, 254)
    scaled = (w * np.exp2(127.0 - byte)[:, None, :]).reshape(k, n).astype(np.float32)
    by_word = np.ascontiguousarray(scaled.reshape(k // 512, 128, 4, n).transpose(0, 1, 3, 2))
    if fmt == "e4m3":
        words = by_word.astype(ml_dtypes.float8_e4m3fn).view(np.uint8)
    else:
        c = by_word.astype(ml_dtypes.float4_e2m1fn).view(np.uint8) & 0xF
        words = (c[..., 0::2] | (c[..., 1::2] << 4)).reshape(k // 512, 128, 2 * n)
    return np.ascontiguousarray(words), np.ascontiguousarray(byte.astype(np.uint8).reshape(k // 512, 16, n))


def unpack_weight(words, scales, fmt):
    g, _, n = scales.shape
    words = np.ascontiguousarray(words).reshape(g, 128, n, -1)
    if fmt == "e4m3":
        vals = words.view(ml_dtypes.float8_e4m3fn).astype(np.float64)
    else:
        nib = np.empty((g, 128, n, 4), np.uint8)
        nib[..., 0::2] = words & 0xF
        nib[..., 1::2] = words >> 4
        vals = E2M1[nib]
    vals = vals * np.repeat(np.exp2(scales.astype(np.float64) - 127.0), 8, axis=1)[..., None]
    return vals.transpose(0, 1, 3, 2).reshape(g * 512, n)


K, T, J, R, O, N = 512, 512, 256, 512, 128, 256


def setup_inputs():
    n = np.random.standard_normal
    idx = np.random.permutation(T)[:J]
    idx2 = np.random.permutation(T)[:J]
    idx3 = np.random.permutation(J)[:O]
    idx4 = np.random.permutation(J)[:O]
    fk = mx_kscale(K)
    fr = mx_kscale(R)
    wp = pack_weight(n((K, R)) * 1 / np.sqrt(K) * fk[:, None] * fr, "e2m1")
    wbp = pack_weight(n((R, N)) * 1 / np.sqrt(R) / fr[:, None], "e2m1")
    return {
        "xf": (n((K, T))).astype(np.float32),
        "fk": (np.random.uniform(0.5, 2.0, (K, 1)) / fk[:, None]).astype(np.float32),
        "w_words": wp[0],
        "w_scales": wp[1],
        "wb_words": wbp[0],
        "wb_scales": wbp[1],
        "bi": (np.random.uniform(-0.5, 0.5, (1, N))).astype(np.float32),
        "offs": striped(idx),
        "offs2": striped(idx2),
        "offs3": striped(idx3),
        "offs4": striped(idx4),
    }


def reference(xf, fk, w_words, w_scales, wb_words, wb_scales, bi, offs, offs2, offs3, offs4):
    idx = unstriped(offs)
    idx2 = unstriped(offs2)
    idx3 = unstriped(offs3)
    idx4 = unstriped(offs4)
    wu = unpack_weight(w_words, w_scales, "e2m1")
    wbu = unpack_weight(wb_words, wb_scales, "e2m1")
    u = (f64(xf)[:, idx] - f64(xf)[:, idx2]) * f64(fk)
    uq = mxq(u, 0, "e4m3")
    a = wu.T @ uq
    ha = np.maximum(a, 0.0)
    hid = ha[:, idx3] - ha[:, idx4]
    hidq = mxq(hid, 0, "e5m2")
    p = hidq.T @ wbu
    ea = np.exp(0.7 * p + f64(bi))
    y = 256.0 * ea / np.sum(ea, axis=1, keepdims=True)
    return y

@@ -1,0 +1,155 @@
+from contextlib import ExitStack
+
+import concourse.mybir as mybir
+
+K, T, J, R, O, N = 512, 512, 256, 512, 128, 256
+FLOPS = 2 * K * R * J + 2 * R * O * N
+
+F32 = mybir.dt.float32
+BF16 = mybir.dt.bfloat16
+I32 = mybir.dt.int32
+U32 = mybir.dt.uint32
+U16 = mybir.dt.uint16
+U8 = mybir.dt.uint8
+E4M3X4 = mybir.dt.float8_e4m3fn_x4
+E5M2X4 = mybir.dt.float8_e5m2_x4
+E2M1X4 = mybir.dt.float4_e2m1fn_x4
+ALU = mybir.AluOpType
+ACT = mybir.ActivationFunctionType
+AXIS = mybir.AxisListType
+
+P = 128
+PACK = 4
+QUAD = 32
+
+
+def load_scale_rows(queue, plane, rows):
+    for q in range(P // QUAD):
+        queue.dma_start(
+            out=plane[QUAD * q : QUAD * q + PACK, :].bitcast(I32),
+            in_=rows[PACK * q : PACK * (q + 1), :].bitcast(I32),
+        )
+
+
+def tile_list_looks_pickgaps_gap_rowshares_kernel(
+    tc, xf, fk, w_words, w_scales, wb_words, wb_scales, bi, offs, offs2, offs3, offs4, out
+):
+    nc = tc.nc
+    with ExitStack() as ctx:
+        lists = ctx.enter_context(tc.tile_pool(name="lists", bufs=1))
+        sb = ctx.enter_context(tc.tile_pool(name="sb", bufs=1))
+        psum = ctx.enter_context(tc.psum_pool(name="psum", bufs=1))
+
+        list1 = lists.tile([P, J // 16], U16, name="list1")
+        list2 = lists.tile([P, J // 16], U16, name="list2")
+        list3 = lists.tile([P, O // 16], U16, name="list3")
+        list4 = lists.tile([P, O // 16], U16, name="list4")
+
+        w_scale_raw = sb.tile([P, R], U8, name="w_scale_raw", align_bytes=64)
+        wb_scale = sb.tile([P, N], U8, name="wb_scale", align_bytes=64)
+        nc.vector.memset(w_scale_raw[:].bitcast(I32), 0)
+        nc.gpsimd.memset(wb_scale[:].bitcast(I32), 0)
+        load_scale_rows(nc.scalar, w_scale_raw, w_scales[0])
+        load_scale_rows(nc.gpsimd, wb_scale, wb_scales[0])
+
+        x_rows = xf.rearrange("(p t) c -> p t c", t=PACK)
+        x_plane = [sb.tile([P, T], F32, name="x_plane%d" % t) for t in range(PACK)]
+        nc.sync.dma_start(list2[:], offs2)
+        nc.sync.dma_start(out=x_plane[0][:], in_=x_rows[:, 0, :])
+        nc.sync.dma_start(list1[:], offs)
+        for t in range(1, PACK):
+            nc.sync.dma_start(out=x_plane[t][:], in_=x_rows[:, t, :])
+        factor = sb.tile([P, PACK], F32, name="factor")
+        nc.sync.dma_start(out=factor[:], in_=fk.rearrange("(p t) one -> p (t one)", t=PACK))
+        w_raw = sb.tile([P, R], U16, name="w_raw", align_bytes=64)
+        nc.sync.dma_start(out=w_raw[:].bitcast(I32), in_=w_words[0].bitcast(I32))
+        nc.sync.dma_start(list4[:], offs4)
+        nc.sync.dma_start(list3[:], offs3)
+        wb_codes = sb.tile([P, N], U16, name="wb_codes", align_bytes=64)
+        nc.sync.dma_start(out=wb_codes[:].bitcast(I32), in_=wb_words[0].bitcast(I32))
+        bias = sb.tile([P, N], F32, name="bias")
+        nc.sync.dma_start(out=bias[:], in_=bi[0].partition_broadcast(P))
+
+        w_scale = sb.tile([P, R], U8, name="w_scale", align_bytes=64)
+        nc.vector.tensor_copy(
+            out=w_scale[:].rearrange("p (t m) -> p t m", t=PACK),
+            in_=w_scale_raw[:].rearrange("p (m t) -> p t m", t=PACK),
+        )
+
+        gap = sb.tile([P, PACK, J], F32, name="gap")
+        for t in range(PACK):
+            second = sb.tile([P, J], F32, name="second%d" % t)
+            nc.scalar.activation(second[:], x_plane[t][:].indirect(list2[:]), ACT.Copy)
+            nc.vector.tensor_tensor(gap[:, t, :], x_plane[t][:].indirect(list1[:]), second[:], ALU.subtract)
+
+        w_codes = sb.tile([P, R], U16, name="w_codes", align_bytes=64)
+        nc.scalar.copy(
+            out=w_codes[:].rearrange("p (t m) -> p t m", t=PACK),
+            in_=w_raw[:].rearrange("p (m t) -> p t m", t=PACK),
+        )
+
+        u_bf = sb.tile([P, J * PACK], BF16, name="u_bf", align_bytes=64)
+        nc.vector.tensor_tensor(
+            u_bf[:].rearrange("p (c i t) -> p c t i", i=4, t=PACK),
+            gap[:].rearrange("p t (c i) -> p c t i", i=4),
+            factor[:].unsqueeze(1).unsqueeze(3).to_broadcast([P, J // 4, PACK, 4]),
+            ALU.mult,
+        )
+        u_codes = sb.tile([P, J], U32, name="u_codes", align_bytes=64)
+        u_scale = sb.tile([P, J], U8, name="u_scale", align_bytes=64)
+        nc.vector.quantize_mx(out=u_codes[:].bitcast(E4M3X4), scales=u_scale[:], in_=u_bf[:])
+
+        hid = sb.tile([P, PACK, O], F32, name="hid")
+        for t in range(PACK):
+            a_sum = psum.tile([P, J], F32, name="a_sum%d" % t)
+            cols = slice(P * t, P * (t + 1))
+            nc.tensor.matmul_mx(
+                out=a_sum[:],
+                lhsT=w_codes[:, cols].bitcast(E2M1X4),
+                lhsT_scale=w_scale[:, cols],
+                rhs=u_codes[:].bitcast(E4M3X4),
+                rhs_scale=u_scale[:],
+                start=True,
+                stop=True,
+            )
+            ha = sb.tile([P, J], F32, name="ha%d" % t)
+            if t % 2 == 0:
+                nc.vector.tensor_scalar(ha[:], a_sum[:], 0.0, None, ALU.max)
+            else:
+                nc.scalar.activation(ha[:], a_sum[:], ACT.Relu)
+            other = sb.tile([P, O], F32, name="other%d" % t)
+            nc.scalar.activation(other[:], ha[:].indirect(list4[:]), ACT.Copy)
+            nc.vector.tensor_tensor(hid[:, t, :], ha[:].indirect(list3[:]), other[:], ALU.subtract)
+
+        hid_bf = sb.tile([P, O * PACK], BF16, name="hid_bf", align_bytes=64)
+        nc.vector.tensor_copy(
+            out=hid_bf[:].rearrange("p (c i t) -> p c t i", i=4, t=PACK),
+            in_=hid[:].rearrange("p t (c i) -> p c t i", i=4),
+        )
+        hid_codes = sb.tile([P, O], U32, name="hid_codes", align_bytes=64)
+        hid_scale = sb.tile([P, O], U8, name="hid_scale", align_bytes=64)
+        nc.vector.quantize_mx(out=hid_codes[:].bitcast(E5M2X4), scales=hid_scale[:], in_=hid_bf[:])
+
+        p_sum = psum.tile([P, N], F32, name="p_sum")
+        nc.tensor.matmul_mx(
+            out=p_sum[:],
+            lhsT=hid_codes[:].bitcast(E5M2X4),
+            lhsT_scale=hid_scale[:],
+            rhs=wb_codes[:].bitcast(E2M1X4),
+            rhs_scale=wb_scale[:],
+            start=True,
+            stop=True,
+        )
+
+        logit = sb.tile([P, N], F32, name="logit")
+        nc.vector.scalar_tensor_tensor(logit[:], p_sum[:], 0.7, bias[:], ALU.mult, ALU.add)
+        neg_top = sb.tile([P, 1], F32, name="neg_top")
+        nc.vector.tensor_reduce(neg_top[:], logit[:], AXIS.X, ALU.max, negate=True)
+        ea = sb.tile([P, N], F32, name="ea")
+        total = sb.tile([P, 1], F32, name="total")
+        nc.scalar.activation(ea[:], logit[:], ACT.Exp, bias=neg_top[:], accum_out=total[:])
+        inverse = sb.tile([P, 1], F32, name="inverse")
+        nc.vector.reciprocal(inverse[:], total[:])
+        shares = sb.tile([P, N], F32, name="shares")
+        nc.vector.tensor_scalar(shares[:], ea[:], inverse[:], 256.0, ALU.mult, ALU.mult)
+        nc.sync.dma_start(out=out, in_=shares[:])

@@ -45,6 +45,11 @@ def tile_list_looks_pickgaps_gap_rowshares_kernel(
         list3 = lists.tile([P, O // 16], U16, name="list3")
         list4 = lists.tile([P, O // 16], U16, name="list4")
 
+        warm_in = sb.tile([P, 1], F32, name="warm_in")
+        warm_out = sb.tile([P, 1], F32, name="warm_out")
+        nc.vector.memset(warm_in[:], 0.0)
+        nc.scalar.activation(warm_out[:], warm_in[:], ACT.Exp)
+
         w_scale_raw = sb.tile([P, R], U8, name="w_scale_raw", align_bytes=64)
         wb_scale = sb.tile([P, N], U8, name="wb_scale", align_bytes=64)
         nc.vector.memset(w_scale_raw[:].bitcast(I32), 0)

@@ -21,10 +21,11 @@ AXIS = mybir.AxisListType
 P = 128
 PACK = 4
 QUAD = 32
+HALF = J // 2
 
 
-def load_scale_rows(queue, plane, rows):
-    for q in range(P // QUAD):
+def load_scale_rows(queue, plane, rows, quadrants):
+    for q in quadrants:
         queue.dma_start(
             out=plane[QUAD * q : QUAD * q + PACK, :].bitcast(I32),
             in_=rows[PACK * q : PACK * (q + 1), :].bitcast(I32),
@@ -45,23 +46,21 @@ def tile_list_looks_pickgaps_gap_rowshares_kernel(
         list3 = lists.tile([P, O // 16], U16, name="list3")
         list4 = lists.tile([P, O // 16], U16, name="list4")
 
+        w_scale_raw = sb.tile([P, R], U8, name="w_scale_raw", align_bytes=64)
+        wb_scale = sb.tile([P, N], U8, name="wb_scale", align_bytes=64)
+        nc.gpsimd.memset(w_scale_raw[:].bitcast(I32), 0)
         warm_in = sb.tile([P, 1], F32, name="warm_in")
         warm_out = sb.tile([P, 1], F32, name="warm_out")
         nc.vector.memset(warm_in[:], 0.0)
         nc.scalar.activation(warm_out[:], warm_in[:], ACT.Exp)
 
-        w_scale_raw = sb.tile([P, R], U8, name="w_scale_raw", align_bytes=64)
-        wb_scale = sb.tile([P, N], U8, name="wb_scale", align_bytes=64)
-        nc.vector.memset(w_scale_raw[:].bitcast(I32), 0)
-        nc.gpsimd.memset(wb_scale[:].bitcast(I32), 0)
-        load_scale_rows(nc.scalar, w_scale_raw, w_scales[0])
-        load_scale_rows(nc.gpsimd, wb_scale, wb_scales[0])
-
+        nc.vector.memset(wb_scale[:].bitcast(I32), 0)
         x_rows = xf.rearrange("(p t) c -> p t c", t=PACK)
         x_plane = [sb.tile([P, T], F32, name="x_plane%d" % t) for t in range(PACK)]
         nc.sync.dma_start(list2[:], offs2)
-        nc.sync.dma_start(out=x_plane[0][:], in_=x_rows[:, 0, :])
         nc.sync.dma_start(list1[:], offs)
+        nc.sync.dma_start(out=x_plane[0][:], in_=x_rows[:, 0, :])
+        load_scale_rows(nc.sync, w_scale_raw, w_scales[0], range(4))
         for t in range(1, PACK):
             nc.sync.dma_start(out=x_plane[t][:], in_=x_rows[:, t, :])
         factor = sb.tile([P, PACK], F32, name="factor")
@@ -72,6 +71,7 @@ def tile_list_looks_pickgaps_gap_rowshares_kernel(
         nc.sync.dma_start(list3[:], offs3)
         wb_codes = sb.tile([P, N], U16, name="wb_codes", align_bytes=64)
         nc.sync.dma_start(out=wb_codes[:].bitcast(I32), in_=wb_words[0].bitcast(I32))
+        load_scale_rows(nc.sync, wb_scale, wb_scales[0], range(4))
         bias = sb.tile([P, N], F32, name="bias")
         nc.sync.dma_start(out=bias[:], in_=bi[0].partition_broadcast(P))
 
@@ -81,55 +81,76 @@ def tile_list_looks_pickgaps_gap_rowshares_kernel(
             in_=w_scale_raw[:].rearrange("p (m t) -> p t m", t=PACK),
         )
 
-        gap = sb.tile([P, PACK, J], F32, name="gap")
-        for t in range(PACK):
-            second = sb.tile([P, J], F32, name="second%d" % t)
-            nc.scalar.activation(second[:], x_plane[t][:].indirect(list2[:]), ACT.Copy)
-            nc.vector.tensor_tensor(gap[:, t, :], x_plane[t][:].indirect(list1[:]), second[:], ALU.subtract)
-
+        gap = [sb.tile([P, PACK, HALF], F32, name="gap%d" % h) for h in range(2)]
+        u_bf = [sb.tile([P, HALF * PACK], BF16, name="u_bf%d" % h, align_bytes=64) for h in range(2)]
+        u_codes = [sb.tile([P, HALF], U32, name="u_codes%d" % h, align_bytes=64) for h in range(2)]
+        u_scale = [sb.tile([P, HALF], U8, name="u_scale%d" % h, align_bytes=64) for h in range(2)]
         w_codes = sb.tile([P, R], U16, name="w_codes", align_bytes=64)
+        ha = [sb.tile([P, J], F32, name="ha%d" % t) for t in range(PACK)]
+
+        def take_gap(t, h):
+            cols = slice(h * HALF // 16, (h + 1) * HALF // 16)
+            second = sb.tile([P, HALF], F32, name="second%d_%d" % (t, h))
+            nc.scalar.activation(second[:], x_plane[t][:].indirect(list2[:, cols]), ACT.Copy)
+            nc.vector.tensor_tensor(gap[h][:, t, :], x_plane[t][:].indirect(list1[:, cols]), second[:], ALU.subtract)
+
+        def scale_and_round(h):
+            nc.vector.tensor_tensor(
+                u_bf[h][:].rearrange("p (c i t) -> p c t i", i=4, t=PACK),
+                gap[h][:].rearrange("p t (c i) -> p c t i", i=4),
+                factor[:].unsqueeze(1).unsqueeze(3).to_broadcast([P, HALF // 4, PACK, 4]),
+                ALU.mult,
+            )
+
+        def quantise_u(h):
+            nc.vector.quantize_mx(out=u_codes[h][:].bitcast(E4M3X4), scales=u_scale[h][:], in_=u_bf[h][:])
+
+        def first_product(a_sum, t, h):
+            cols = slice(P * t, P * (t + 1))
+            nc.tensor.matmul_mx(
+                out=a_sum,
+                lhsT=w_codes[:, cols].bitcast(E2M1X4),
+                lhsT_scale=w_scale[:, cols],
+                rhs=u_codes[h][:].bitcast(E4M3X4),
+                rhs_scale=u_scale[h][:],
+                start=True,
+                stop=True,
+            )
+
+        for t in range(PACK):
+            for h in range(2):
+                take_gap(t, h)
+        for h in range(2):
+            scale_and_round(h)
+        for h in range(2):
+            quantise_u(h)
         nc.scalar.copy(
             out=w_codes[:].rearrange("p (t m) -> p t m", t=PACK),
             in_=w_raw[:].rearrange("p (m t) -> p t m", t=PACK),
         )
 
-        u_bf = sb.tile([P, J * PACK], BF16, name="u_bf", align_bytes=64)
-        nc.vector.tensor_tensor(
-            u_bf[:].rearrange("p (c i t) -> p c t i", i=4, t=PACK),
-            gap[:].rearrange("p t (c i) -> p c t i", i=4),
-            factor[:].unsqueeze(1).unsqueeze(3).to_broadcast([P, J // 4, PACK, 4]),
-            ALU.mult,
-        )
-        u_codes = sb.tile([P, J], U32, name="u_codes", align_bytes=64)
-        u_scale = sb.tile([P, J], U8, name="u_scale", align_bytes=64)
-        nc.vector.quantize_mx(out=u_codes[:].bitcast(E4M3X4), scales=u_scale[:], in_=u_bf[:])
-
-        hid = sb.tile([P, PACK, O], F32, name="hid")
+        a_sum = [psum.tile([P, J], F32, name="a_sum%d" % t) for t in range(PACK)]
         for t in range(PACK):
-            a_sum = psum.tile([P, J], F32, name="a_sum%d" % t)
-            cols = slice(P * t, P * (t + 1))
-            nc.tensor.matmul_mx(
-                out=a_sum[:],
-                lhsT=w_codes[:, cols].bitcast(E2M1X4),
-                lhsT_scale=w_scale[:, cols],
-                rhs=u_codes[:].bitcast(E4M3X4),
-                rhs_scale=u_scale[:],
-                start=True,
-                stop=True,
-            )
-            ha = sb.tile([P, J], F32, name="ha%d" % t)
-            if t % 2 == 0:
-                nc.vector.tensor_scalar(ha[:], a_sum[:], 0.0, None, ALU.max)
+            for h in range(2):
+                first_product(a_sum[t][:, h * HALF : (h + 1) * HALF], t, h)
+        for t in range(PACK):
+            if t in (0, PACK - 1):
+                nc.scalar.activation(ha[t][:], a_sum[t][:], ACT.Relu)
             else:
-                nc.scalar.activation(ha[:], a_sum[:], ACT.Relu)
-            other = sb.tile([P, O], F32, name="other%d" % t)
-            nc.scalar.activation(other[:], ha[:].indirect(list4[:]), ACT.Copy)
-            nc.vector.tensor_tensor(hid[:, t, :], ha[:].indirect(list3[:]), other[:], ALU.subtract)
+                nc.vector.tensor_scalar(ha[t][:], a_sum[t][:], 0.0, None, ALU.max)
+
+        picked3 = sb.tile([P, PACK, O], F32, name="picked3")
+        picked4 = sb.tile([P, PACK, O], F32, name="picked4")
+        for t in range(PACK):
+            nc.scalar.activation(picked4[:, t, :], ha[t][:].indirect(list4[:]), ACT.Copy)
+            nc.vector.tensor_copy(picked3[:, t, :], ha[t][:].indirect(list3[:]))
 
         hid_bf = sb.tile([P, O * PACK], BF16, name="hid_bf", align_bytes=64)
-        nc.vector.tensor_copy(
-            out=hid_bf[:].rearrange("p (c i t) -> p c t i", i=4, t=PACK),
-            in_=hid[:].rearrange("p t (c i) -> p c t i", i=4),
+        nc.vector.tensor_tensor(
+            hid_bf[:].rearrange("p (c i t) -> p c t i", i=4, t=PACK),
+            picked3[:].rearrange("p t (c i) -> p c t i", i=4),
+            picked4[:].rearrange("p t (c i) -> p c t i", i=4),
+            ALU.subtract,
         )
         hid_codes = sb.tile([P, O], U32, name="hid_codes", align_bytes=64)
         hid_scale = sb.tile([P, O], U8, name="hid_scale", align_bytes=64)

from contextlib import ExitStack

import concourse.mybir as mybir

K, T, J, R, O, N = 512, 512, 256, 512, 128, 256
FLOPS = 2 * K * R * J + 2 * R * O * N

F32 = mybir.dt.float32
BF16 = mybir.dt.bfloat16
I32 = mybir.dt.int32
U32 = mybir.dt.uint32
U16 = mybir.dt.uint16
U8 = mybir.dt.uint8
E4M3X4 = mybir.dt.float8_e4m3fn_x4
E5M2X4 = mybir.dt.float8_e5m2_x4
E2M1X4 = mybir.dt.float4_e2m1fn_x4
ALU = mybir.AluOpType
ACT = mybir.ActivationFunctionType
AXIS = mybir.AxisListType

P = 128
PACK = 4
QUAD = 32
HALF = J // 2


def load_scale_rows(queue, plane, rows, quadrants):
    for q in quadrants:
        queue.dma_start(
            out=plane[QUAD * q : QUAD * q + PACK, :].bitcast(I32),
            in_=rows[PACK * q : PACK * (q + 1), :].bitcast(I32),
        )


def tile_list_looks_pickgaps_gap_rowshares_kernel(
    tc, xf, fk, w_words, w_scales, wb_words, wb_scales, bi, offs, offs2, offs3, offs4, out
):
    nc = tc.nc
    with ExitStack() as ctx:
        lists = ctx.enter_context(tc.tile_pool(name="lists", bufs=1))
        sb = ctx.enter_context(tc.tile_pool(name="sb", bufs=1))
        psum = ctx.enter_context(tc.psum_pool(name="psum", bufs=1))

        list1 = lists.tile([P, J // 16], U16, name="list1")
        list2 = lists.tile([P, J // 16], U16, name="list2")
        list3 = lists.tile([P, O // 16], U16, name="list3")
        list4 = lists.tile([P, O // 16], U16, name="list4")

        w_scale_raw = sb.tile([P, R], U8, name="w_scale_raw", align_bytes=64)
        wb_scale = sb.tile([P, N], U8, name="wb_scale", align_bytes=64)
        nc.gpsimd.memset(w_scale_raw[:].bitcast(I32), 0)
        warm_in = sb.tile([P, 1], F32, name="warm_in")
        warm_out = sb.tile([P, 1], F32, name="warm_out")
        nc.vector.memset(warm_in[:], 0.0)
        nc.scalar.activation(warm_out[:], warm_in[:], ACT.Exp)

        nc.vector.memset(wb_scale[:].bitcast(I32), 0)
        x_rows = xf.rearrange("(p t) c -> p t c", t=PACK)
        x_plane = [sb.tile([P, T], F32, name="x_plane%d" % t) for t in range(PACK)]
        nc.sync.dma_start(list2[:], offs2)
        nc.sync.dma_start(list1[:], offs)
        nc.sync.dma_start(out=x_plane[0][:], in_=x_rows[:, 0, :])
        load_scale_rows(nc.sync, w_scale_raw, w_scales[0], range(4))
        for t in range(1, PACK):
            nc.sync.dma_start(out=x_plane[t][:], in_=x_rows[:, t, :])
        factor = sb.tile([P, PACK], F32, name="factor")
        nc.sync.dma_start(out=factor[:], in_=fk.rearrange("(p t) one -> p (t one)", t=PACK))
        w_raw = sb.tile([P, R], U16, name="w_raw", align_bytes=64)
        nc.sync.dma_start(out=w_raw[:].bitcast(I32), in_=w_words[0].bitcast(I32))
        nc.sync.dma_start(list4[:], offs4)
        nc.sync.dma_start(list3[:], offs3)
        wb_codes = sb.tile([P, N], U16, name="wb_codes", align_bytes=64)
        nc.sync.dma_start(out=wb_codes[:].bitcast(I32), in_=wb_words[0].bitcast(I32))
        load_scale_rows(nc.sync, wb_scale, wb_scales[0], range(4))
        bias = sb.tile([P, N], F32, name="bias")
        nc.sync.dma_start(out=bias[:], in_=bi[0].partition_broadcast(P))

        w_scale = sb.tile([P, R], U8, name="w_scale", align_bytes=64)
        nc.vector.tensor_copy(
            out=w_scale[:].rearrange("p (t m) -> p t m", t=PACK),
            in_=w_scale_raw[:].rearrange("p (m t) -> p t m", t=PACK),
        )

        gap = [sb.tile([P, PACK, HALF], F32, name="gap%d" % h) for h in range(2)]
        u_bf = [sb.tile([P, HALF * PACK], BF16, name="u_bf%d" % h, align_bytes=64) for h in range(2)]
        u_codes = [sb.tile([P, HALF], U32, name="u_codes%d" % h, align_bytes=64) for h in range(2)]
        u_scale = [sb.tile([P, HALF], U8, name="u_scale%d" % h, align_bytes=64) for h in range(2)]
        w_codes = sb.tile([P, R], U16, name="w_codes", align_bytes=64)
        ha = [sb.tile([P, J], F32, name="ha%d" % t) for t in range(PACK)]

        def take_gap(t, h):
            cols = slice(h * HALF // 16, (h + 1) * HALF // 16)
            second = sb.tile([P, HALF], F32, name="second%d_%d" % (t, h))
            nc.scalar.activation(second[:], x_plane[t][:].indirect(list2[:, cols]), ACT.Copy)
            nc.vector.tensor_tensor(gap[h][:, t, :], x_plane[t][:].indirect(list1[:, cols]), second[:], ALU.subtract)

        def scale_and_round(h):
            nc.vector.tensor_tensor(
                u_bf[h][:].rearrange("p (c i t) -> p c t i", i=4, t=PACK),
                gap[h][:].rearrange("p t (c i) -> p c t i", i=4),
                factor[:].unsqueeze(1).unsqueeze(3).to_broadcast([P, HALF // 4, PACK, 4]),
                ALU.mult,
            )

        def quantise_u(h):
            nc.vector.quantize_mx(out=u_codes[h][:].bitcast(E4M3X4), scales=u_scale[h][:], in_=u_bf[h][:])

        def first_product(a_sum, t, h):
            cols = slice(P * t, P * (t + 1))
            nc.tensor.matmul_mx(
                out=a_sum,
                lhsT=w_codes[:, cols].bitcast(E2M1X4),
                lhsT_scale=w_scale[:, cols],
                rhs=u_codes[h][:].bitcast(E4M3X4),
                rhs_scale=u_scale[h][:],
                start=True,
                stop=True,
            )

        for t in range(PACK):
            for h in range(2):
                take_gap(t, h)
        for h in range(2):
            scale_and_round(h)
        for h in range(2):
            quantise_u(h)
        nc.scalar.copy(
            out=w_codes[:].rearrange("p (t m) -> p t m", t=PACK),
            in_=w_raw[:].rearrange("p (m t) -> p t m", t=PACK),
        )

        a_sum = [psum.tile([P, J], F32, name="a_sum%d" % t) for t in range(PACK)]
        for t in range(PACK):
            for h in range(2):
                first_product(a_sum[t][:, h * HALF : (h + 1) * HALF], t, h)
        for t in range(PACK):
            if t in (0, PACK - 1):
                nc.scalar.activation(ha[t][:], a_sum[t][:], ACT.Relu)
            else:
                nc.vector.tensor_scalar(ha[t][:], a_sum[t][:], 0.0, None, ALU.max)

        picked3 = sb.tile([P, PACK, O], F32, name="picked3")
        picked4 = sb.tile([P, PACK, O], F32, name="picked4")
        for t in range(PACK):
            nc.scalar.activation(picked4[:, t, :], ha[t][:].indirect(list4[:]), ACT.Copy)
            nc.vector.tensor_copy(picked3[:, t, :], ha[t][:].indirect(list3[:]))

        hid_bf = sb.tile([P, O * PACK], BF16, name="hid_bf", align_bytes=64)
        nc.vector.tensor_tensor(
            hid_bf[:].rearrange("p (c i t) -> p c t i", i=4, t=PACK),
            picked3[:].rearrange("p t (c i) -> p c t i", i=4),
            picked4[:].rearrange("p t (c i) -> p c t i", i=4),
            ALU.subtract,
        )
        hid_codes = sb.tile([P, O], U32, name="hid_codes", align_bytes=64)
        hid_scale = sb.tile([P, O], U8, name="hid_scale", align_bytes=64)
        nc.vector.quantize_mx(out=hid_codes[:].bitcast(E5M2X4), scales=hid_scale[:], in_=hid_bf[:])

        p_sum = psum.tile([P, N], F32, name="p_sum")
        nc.tensor.matmul_mx(
            out=p_sum[:],
            lhsT=hid_codes[:].bitcast(E5M2X4),
            lhsT_scale=hid_scale[:],
            rhs=wb_codes[:].bitcast(E2M1X4),
            rhs_scale=wb_scale[:],
            start=True,
            stop=True,
        )

        logit = sb.tile([P, N], F32, name="logit")
        nc.vector.scalar_tensor_tensor(logit[:], p_sum[:], 0.7, bias[:], ALU.mult, ALU.add)
        neg_top = sb.tile([P, 1], F32, name="neg_top")
        nc.vector.tensor_reduce(neg_top[:], logit[:], AXIS.X, ALU.max, negate=True)
        ea = sb.tile([P, N], F32, name="ea")
        total = sb.tile([P, 1], F32, name="total")
        nc.scalar.activation(ea[:], logit[:], ACT.Exp, bias=neg_top[:], accum_out=total[:])
        inverse = sb.tile([P, 1], F32, name="inverse")
        nc.vector.reciprocal(inverse[:], total[:])
        shares = sb.tile([P, N], F32, name="shares")
        nc.vector.tensor_scalar(shares[:], ea[:], inverse[:], 256.0, ALU.mult, ALU.mult)
        nc.sync.dma_start(out=out, in_=shares[:])
